import numpy as np
import ml_dtypes


def mxq(x, axis, fmt="e4m3"):
    dtype, down = {"e4m3": (ml_dtypes.float8_e4m3fn, 7), "e5m2": (ml_dtypes.float8_e5m2, 14)}[fmt]
    v = np.moveaxis(np.asarray(x, np.float32).astype(ml_dtypes.bfloat16).astype(np.float64), axis, -1)
    blocks = v.reshape(v.shape[:-1] + (-1, 32))
    amax = np.abs(blocks).max(-1, keepdims=True)
    byte = np.maximum(np.where(amax > 0, np.frexp(amax)[1] - 1 + 127, 0) - down, 1)
    scale = np.exp2(byte - 127.0)
    codes = (blocks / scale).astype(np.float32).astype(dtype).astype(np.float64)
    return np.moveaxis((codes * scale).reshape(v.shape), -1, axis)


WIDE = False


def mx_kscale(k):
    if not WIDE:
        return np.ones(k)
    levels = np.array([30, -30])
    if k % 512:
        return np.exp2(np.random.permutation(np.resize(levels, k // 32))).repeat(32)
    a = np.empty((k // 512, 16))
    for p in range(k // 512):
        a[p, :8] = np.random.permutation(np.resize(levels, 8))
        for g in range(8):
            far = levels[np.abs(levels - a[p, g]) >= 10]
            a[p, g + 8] = far[np.random.randint(len(far))]
    return np.exp2(a.ravel()).repeat(32)


def f64(x):
    return np.asarray(x).astype(np.float64)


def striped(idx):
    return np.tile(np.asarray(idx).reshape(-1, 16).T, (8, 1)).astype(np.uint16)


def unstriped(offs):
    return offs[:16].T.reshape(-1).astype(np.int64)


E2M1 = np.array([0.0, 0.5, 1.0, 1.5, 2.0, 3.0, 4.0, 6.0, -0.0, -0.5, -1.0, -1.5, -2.0, -3.0, -4.0, -6.0])


def pack_weight(w, fmt):
    k, n = w.shape
    w = f64(np.asarray(w, np.float32).astype(ml_dtypes.bfloat16)).reshape(k // 32, 32, n)
    amax = np.abs(w).max(1)
    if fmt in ("e4m3", "e5m2"):
        byte = np.frexp(amax)[1] - 1 + 127 - (7 if fmt == "e4m3" else 14)
    else:
        mant, ex = np.frexp(amax / 6.0)
        byte = np.where(mant > 0.5, ex, ex - 1) + 127
    byte = np.clip(np.where(amax > 0, byte, 1), 1, 254)
    scaled = (w * np.exp2(127.0 - byte)[:, None, :]).reshape(k, n).astype(np.float32)
    by_word = np.ascontiguousarray(scaled.reshape(k // 512, 128, 4, n).transpose(0, 1, 3, 2))
    if fmt in ("e4m3", "e5m2"):
        words = by_word.astype(ml_dtypes.float8_e4m3fn if fmt == "e4m3" else ml_dtypes.float8_e5m2).view(np.uint8)
    else:
        c = by_word.astype(ml_dtypes.float4_e2m1fn).view(np.uint8) & 0xF
        words = (c[..., 0::2] | (c[..., 1::2] << 4)).reshape(k // 512, 128, 2 * n)
    return np.ascontiguousarray(words), np.ascontiguousarray(byte.astype(np.uint8).reshape(k // 512, 16, n))


def unpack_weight(words, scales, fmt):
    g, _, n = scales.shape
    words = np.ascontiguousarray(words).reshape(g, 128, n, -1)
    if fmt in ("e4m3", "e5m2"):
        vals = words.view(ml_dtypes.float8_e4m3fn if fmt == "e4m3" else ml_dtypes.float8_e5m2).astype(np.float64)
    else:
        nib = np.empty((g, 128, n, 4), np.uint8)
        nib[..., 0::2] = words & 0xF
        nib[..., 1::2] = words >> 4
        vals = E2M1[nib]
    vals = vals * np.repeat(np.exp2(scales.astype(np.float64) - 127.0), 8, axis=1)[..., None]
    return vals.transpose(0, 1, 3, 2).reshape(g * 512, n)


K, T, J, R, V, N, U, E = 512, 1024, 256, 512, 1024, 256, 128, 512


def setup_inputs():
    n = np.random.standard_normal
    idx = np.random.permutation(V)[:R]
    idx2 = np.random.permutation(T)[:J]
    idx3 = np.random.permutation(J)[:U]
    idx4 = np.random.permutation(E)[:U]
    idx5 = np.random.permutation(E)[:J]
    fk = mx_kscale(K)
    fr = mx_kscale(R)
    tr = np.ones(V)
    tr[idx] = fr
    xtp = pack_weight(n((K, T)) / fk[:, None], "e5m2")
    wtp = pack_weight(n((K, V)) * 1 / np.sqrt(K) * fk[:, None] * tr, "e2m1")
    w2p = pack_weight(n((K, R)) * 1 / np.sqrt(K) * fk[:, None] * fr, "e4m3")
    wbp = pack_weight(n((R, N)) * 1 / np.sqrt(R) / fr[:, None], "e2m1")
    wcp = pack_weight(n((R, N)) * 1 / np.sqrt(R) / fr[:, None], "e4m3")
    return {
        "xt_words": xtp[0],
        "xt_scales": xtp[1],
        "wt_words": wtp[0],
        "wt_scales": wtp[1],
        "w2_words": w2p[0],
        "w2_scales": w2p[1],
        "wb_words": wbp[0],
        "wb_scales": wbp[1],
        "wc_words": wcp[0],
        "wc_scales": wcp[1],
        "offs": striped(idx),
        "offs2": striped(idx2),
        "offs3": striped(idx3),
        "offs4": striped(idx4),
        "offs5": striped(idx5),
    }


def reference(xt_words, xt_scales, wt_words, wt_scales, w2_words, w2_scales, wb_words, wb_scales, wc_words, wc_scales, offs, offs2, offs3, offs4, offs5):
    idx = unstriped(offs)
    idx2 = unstriped(offs2)
    idx3 = unstriped(offs3)
    idx4 = unstriped(offs4)
    idx5 = unstriped(offs5)
    xtu = unpack_weight(xt_words, xt_scales, "e5m2")
    wtu = unpack_weight(wt_words, wt_scales, "e2m1")
    w2u = unpack_weight(w2_words, w2_scales, "e4m3")
    wbu = unpack_weight(wb_words, wb_scales, "e2m1")
    wcu = unpack_weight(wc_words, wc_scales, "e4m3")
    wtidxg = wtu[:, idx]
    xtidx2g = xtu[:, idx2]
    a = wtidxg.T @ xtidx2g
    b = w2u.T @ xtidx2g
    hid = np.maximum(a, b)
    hidq = mxq(hid, 0, "e4m3")
    p = wbu.T @ hidq
    q = wcu.T @ hidq
    lq = q[:, 0:1]
    m0 = p[:, idx3] * lq
    pw = np.zeros((N, E))
    pw[:, idx4] = m0
    pv = np.zeros((N, E))
    pv[:, idx5] = q
    y = pw + pv
    return y

@@ -1,0 +1,174 @@
+from contextlib import ExitStack
+
+import concourse.mybir as mybir
+from concourse.masks import make_identity
+
+K, T, J, R, V, N, U, E = 512, 1024, 256, 512, 1024, 256, 128, 512
+FLOPS = 2 * (2 * K * R * J + 2 * R * N * J)
+
+F32 = mybir.dt.float32
+BF16 = mybir.dt.bfloat16
+I32 = mybir.dt.int32
+U32 = mybir.dt.uint32
+U16 = mybir.dt.uint16
+U8 = mybir.dt.uint8
+E4M3 = mybir.dt.float8_e4m3fn_x4
+E5M2 = mybir.dt.float8_e5m2_x4
+E2M1 = mybir.dt.float4_e2m1fn_x4
+COPY = mybir.ActivationFunctionType.Copy
+
+P = 128
+HALF_R = R // 2
+LIST_COL = 16
+
+
+def tile_list_outcomepages_storeleads_kernel(
+    tc, xt_words, xt_scales, wt_words, wt_scales, w2_words, w2_scales,
+    wb_words, wb_scales, wc_words, wc_scales, offs, offs2, offs3, offs4, offs5, out,
+):
+    nc = tc.nc
+    with ExitStack() as ctx:
+        sb = ctx.enter_context(tc.tile_pool(name="sb", bufs=1))
+        ps = ctx.enter_context(tc.psum_pool(name="ps", bufs=1))
+
+        def tile(name, shape, dtype):
+            return sb.tile(shape, dtype, name=name, align_bytes=64)
+
+        l_r = tile("l_r", [P, R // LIST_COL], U16)
+        l_j = tile("l_j", [P, J // LIST_COL], U16)
+        l_u = tile("l_u", [P, U // LIST_COL], U16)
+        l_pw = tile("l_pw", [P, U // LIST_COL], U16)
+        l_pv = tile("l_pv", [P, J // LIST_COL], U16)
+
+        xs_stage = tile("xs_stage", [64, 2, T // 4], I32)
+        xs_all = tile("xs_all", [P, T], U8)
+        xw_all = tile("xw_all", [P, T], U32)
+        ws_all = tile("ws_all", [P, V], U8)
+        ww_all = tile("ww_all", [P, V], U16)
+        w2s = tile("w2s", [P, 2, R], U8)
+        w2w = tile("w2w", [P, R], U32)
+        wcs = tile("wcs", [P, N], U8)
+        wbs = tile("wbs", [P, N], U8)
+        wcw = tile("wcw", [P, N], U32)
+        wbw = tile("wbw", [P, 2 * N], U8)
+        pv = [tile(f"pv{n}", [P, E], F32) for n in range(2)]
+        pw = [tile(f"pw{n}", [P, E], F32) for n in range(2)]
+        ident = tile("ident", [P, P], F32)
+
+        nc.vector.memset(xs_stage[:], 0)
+        nc.vector.memset(w2s[:].rearrange("p h c -> p (h c)").bitcast(I32), 0)
+        nc.vector.memset(ws_all[:].bitcast(I32), 0)
+        nc.vector.memset(wcs[:].bitcast(I32), 0)
+        nc.vector.memset(wbs[:].bitcast(I32), 0)
+        for page in pv + pw:
+            nc.vector.memset(page[:], 0.0)
+        make_identity(nc, ident[:])
+
+        def load_rows_direct(plane, scales):
+            rows = scales[0].bitcast(I32)
+            for q in range(4):
+                nc.sync.dma_start(plane[32 * q : 32 * q + 4, :].bitcast(I32), rows[4 * q : 4 * q + 4, :])
+
+        def load_rows_paired(stage, scales):
+            rows = scales[0].bitcast(I32).rearrange("(h q r) c -> q r h c", h=2, q=2)
+            for q in range(2):
+                nc.scalar.dma_start(stage[32 * q : 32 * q + 4, :, :], rows[q])
+
+        nc.sync.dma_start(l_j[:], offs2)
+        load_rows_paired(xs_stage, xt_scales)
+        nc.sync.dma_start(l_r[:], offs)
+        nc.sync.dma_start(xw_all[:].bitcast(I32), xt_words[0].rearrange("p c t -> p (c t)").bitcast(I32))
+        load_rows_paired(w2s[:].bitcast(I32), w2_scales)
+        nc.sync.dma_start(ww_all[:].bitcast(I32), wt_words[0].bitcast(I32))
+        nc.sync.dma_start(w2w[:].bitcast(I32), w2_words[0].rearrange("p c t -> p (c t)").bitcast(I32))
+        load_rows_direct(ws_all, wt_scales)
+        nc.sync.dma_start(wcw[:].bitcast(I32), wc_words[0].rearrange("p c t -> p (c t)").bitcast(I32))
+        nc.sync.dma_start(wbw[:].bitcast(I32), wb_words[0].bitcast(I32))
+        load_rows_direct(wcs, wc_scales)
+        nc.sync.dma_start(l_pv[:], offs5)
+        nc.sync.dma_start(l_u[:], offs3)
+        nc.sync.dma_start(l_pw[:], offs4)
+        load_rows_direct(wbs, wb_scales)
+
+        for h in range(2):
+            nc.vector.tensor_copy(xs_all[64 * h : 64 * h + 64, :].bitcast(I32), xs_stage[:, h, :])
+        xs = tile("xs", [P, J], U8)
+        xw = tile("xw", [P, J], U32)
+        nc.vector.tensor_copy(xs[:], xs_all[:].indirect(l_j[:]))
+        nc.vector.tensor_copy(xw[:], xw_all[:].indirect(l_j[:]))
+        nc.vector.tensor_copy(w2s[64:128, 0, :].bitcast(I32), w2s[0:64, 1, :].bitcast(I32))
+
+        ww, ws = [], []
+        for h in range(2):
+            cols = slice(h * HALF_R // LIST_COL, (h + 1) * HALF_R // LIST_COL)
+            ww.append(tile(f"ww{h}", [P, HALF_R], U16))
+            nc.vector.tensor_copy(ww[h][:], ww_all[:].indirect(l_r[:, cols]))
+        for h in range(2):
+            cols = slice(h * HALF_R // LIST_COL, (h + 1) * HALF_R // LIST_COL)
+            ws.append(tile(f"ws{h}", [P, HALF_R], U8))
+            nc.vector.tensor_copy(ws[h][:], ws_all[:].indirect(l_r[:, cols]))
+
+        def x_side(jh):
+            cols = slice(jh * P, (jh + 1) * P)
+            return dict(lhsT=xw[:, cols].bitcast(E5M2), lhsT_scale=xs[:, cols])
+
+        b_sb = []
+        for h in range(2):
+            cols = slice(h * HALF_R, (h + 1) * HALF_R)
+            b_ps = ps.tile([P, 2, HALF_R], F32, name=f"b_ps{h}", tag=f"bank_b{h}")
+            for jh in range(2):
+                nc.tensor.matmul_mx(b_ps[:, jh, :], rhs=w2w[:, cols].bitcast(E4M3), rhs_scale=w2s[:, 0, cols],
+                                    start=True, stop=True, **x_side(jh))
+            b_sb.append(tile(f"b_sb{h}", [P, 2, 2, 64, 2], F32))
+            nc.scalar.copy(b_sb[h][:], b_ps[:].rearrange("p j (m u e) -> p j u m e", u=2, e=2))
+
+        hid = [tile(f"hid{jh}", [P, 2, P, 2], BF16) for jh in range(2)]
+        for h in range(2):
+            a_ps = ps.tile([P, 2, HALF_R], F32, name=f"a_ps{h}", tag=f"bank_a{h}")
+            for jh in range(2):
+                nc.tensor.matmul_mx(a_ps[:, jh, :], rhs=ww[h][:].bitcast(E2M1), rhs_scale=ws[h][:],
+                                    start=True, stop=True, **x_side(jh))
+            for jh in range(2):
+                nc.vector.tensor_tensor(
+                    hid[jh][:, :, 64 * h : 64 * h + 64, :],
+                    a_ps[:, jh, :].rearrange("p (m u e) -> p u m e", u=2, e=2),
+                    b_sb[h][:, jh, :, :, :],
+                    mybir.AluOpType.max,
+                )
+
+        p_ps = [ps.tile([P, 2, P], F32, name=f"p_ps{n}", tag=f"bank_p{n}") for n in range(2)]
+        q_sb = []
+        for jh in range(2):
+            words = hid[jh][:].rearrange("p u m e -> p (u m e)").bitcast(F32)
+            t_ps = ps.tile([P, 2, P], F32, name=f"t_ps{jh}", tag=f"bank_b{jh}")
+            for u in range(2):
+                nc.tensor.transpose(t_ps[:, u, :], words[:, u * P : (u + 1) * P], ident[:])
+            hid_t = tile(f"hid_t{jh}", [P, 4 * P], BF16)
+            nc.scalar.copy(hid_t[:].bitcast(F32).rearrange("p (j u) -> p j u", u=2), t_ps[:].rearrange("p u j -> p j u"))
+            hw = tile(f"hw{jh}", [P, P], U32)
+            hs = tile(f"hs{jh}", [P, P], U8)
+            nc.vector.quantize_mx(hw[:].bitcast(E4M3), hs[:], hid_t[:])
+            h_side = dict(rhs=hw[:].bitcast(E4M3), rhs_scale=hs[:], start=True, stop=True)
+            q_ps = ps.tile([P, 2, P], F32, name=f"q_ps{jh}", tag=f"bank_q{jh}")
+            for n in range(2):
+                cols = slice(n * P, (n + 1) * P)
+                nc.tensor.matmul_mx(q_ps[:, n, :], lhsT=wcw[:, cols].bitcast(E4M3), lhsT_scale=wcs[:, cols], **h_side)
+            for n in range(2):
+                cols = slice(n * P, (n + 1) * P)
+                nc.tensor.matmul_mx(p_ps[n][:, jh, :], lhsT=wbw[:, 2 * n * P : 2 * (n + 1) * P].bitcast(E2M1),
+                                    lhsT_scale=wbs[:, cols], **h_side)
+            q_sb.append(tile(f"q_sb{jh}", [P, 2, P], F32))
+            nc.scalar.copy(q_sb[jh][:], q_ps[:])
+
+        for n in range(2):
+            p_sb = tile(f"p_sb{n}", [P, J], F32)
+            nc.scalar.copy(p_sb[:], p_ps[n][:].rearrange("p h j -> p (h j)"))
+            m0 = tile(f"m0_{n}", [P, U], F32)
+            nc.scalar.activation(m0[:], p_sb[:].indirect(l_u[:]), COPY, scale=q_sb[0][:, n, 0:1])
+            nc.scalar.activation(pw[n][:].indirect(l_pw[:]), m0[:], COPY)
+            for jh in range(2):
+                cols = slice(jh * P // LIST_COL, (jh + 1) * P // LIST_COL)
+                nc.vector.tensor_copy(pv[n][:].indirect(l_pv[:, cols]), q_sb[jh][:, n, :])
+            y = tile(f"y{n}", [P, E], F32)
+            nc.vector.tensor_tensor(y[:], pw[n][:], pv[n][:], mybir.AluOpType.add)
+            nc.sync.dma_start(out[n * P : (n + 1) * P, :], y[:])

@@ -31,8 +31,8 @@ def tile_list_outcomepages_storeleads_kernel(
         sb = ctx.enter_context(tc.tile_pool(name="sb", bufs=1))
         ps = ctx.enter_context(tc.psum_pool(name="ps", bufs=1))
 
-        def tile(name, shape, dtype):
-            return sb.tile(shape, dtype, name=name, align_bytes=64)
+        def tile(name, shape, dtype, tag=None):
+            return sb.tile(shape, dtype, name=name, tag=tag or name, align_bytes=64)
 
         l_r = tile("l_r", [P, R // LIST_COL], U16)
         l_j = tile("l_j", [P, J // LIST_COL], U16)
@@ -40,28 +40,25 @@ def tile_list_outcomepages_storeleads_kernel(
         l_pw = tile("l_pw", [P, U // LIST_COL], U16)
         l_pv = tile("l_pv", [P, J // LIST_COL], U16)
 
-        xs_stage = tile("xs_stage", [64, 2, T // 4], I32)
         xs_all = tile("xs_all", [P, T], U8)
         xw_all = tile("xw_all", [P, T], U32)
         ws_all = tile("ws_all", [P, V], U8)
         ww_all = tile("ww_all", [P, V], U16)
         w2s = tile("w2s", [P, 2, R], U8)
         w2w = tile("w2w", [P, R], U32)
-        wcs = tile("wcs", [P, N], U8)
-        wbs = tile("wbs", [P, N], U8)
+        out_scales = tile("out_scales", [P, 2 * N], U8)
+        wcs, wbs = out_scales[:, 0:N], out_scales[:, N : 2 * N]
+        pv = [tile("pv0", [P, E], F32)]
+        pw = []
         wcw = tile("wcw", [P, N], U32)
         wbw = tile("wbw", [P, 2 * N], U8)
-        pv = [tile(f"pv{n}", [P, E], F32) for n in range(2)]
-        pw = [tile(f"pw{n}", [P, E], F32) for n in range(2)]
         ident = tile("ident", [P, P], F32)
 
-        nc.vector.memset(xs_stage[:], 0)
+        nc.vector.memset(xs_all[:].bitcast(I32), 0)
         nc.vector.memset(w2s[:].rearrange("p h c -> p (h c)").bitcast(I32), 0)
         nc.vector.memset(ws_all[:].bitcast(I32), 0)
-        nc.vector.memset(wcs[:].bitcast(I32), 0)
-        nc.vector.memset(wbs[:].bitcast(I32), 0)
-        for page in pv + pw:
-            nc.vector.memset(page[:], 0.0)
+        nc.vector.memset(out_scales[:].bitcast(I32), 0)
+        nc.vector.memset(pv[0][:], 0.0)
         make_identity(nc, ident[:])
 
         def load_rows_direct(plane, scales):
@@ -72,103 +69,101 @@ def tile_list_outcomepages_storeleads_kernel(
         def load_rows_paired(stage, scales):
             rows = scales[0].bitcast(I32).rearrange("(h q r) c -> q r h c", h=2, q=2)
             for q in range(2):
-                nc.scalar.dma_start(stage[32 * q : 32 * q + 4, :, :], rows[q])
+                nc.sync.dma_start(stage[32 * q : 32 * q + 4, :, :], rows[q])
 
-        nc.sync.dma_start(l_j[:], offs2)
-        load_rows_paired(xs_stage, xt_scales)
         nc.sync.dma_start(l_r[:], offs)
-        nc.sync.dma_start(xw_all[:].bitcast(I32), xt_words[0].rearrange("p c t -> p (c t)").bitcast(I32))
-        load_rows_paired(w2s[:].bitcast(I32), w2_scales)
         nc.sync.dma_start(ww_all[:].bitcast(I32), wt_words[0].bitcast(I32))
+        nc.sync.dma_start(l_j[:], offs2)
+        load_rows_direct(xs_all, xt_scales)
+        nc.sync.dma_start(xw_all[:].bitcast(I32), xt_words[0].rearrange("p c t -> p (c t)").bitcast(I32))
         nc.sync.dma_start(w2w[:].bitcast(I32), w2_words[0].rearrange("p c t -> p (c t)").bitcast(I32))
+        load_rows_paired(w2s[:].bitcast(I32), w2_scales)
         load_rows_direct(ws_all, wt_scales)
         nc.sync.dma_start(wcw[:].bitcast(I32), wc_words[0].rearrange("p c t -> p (c t)").bitcast(I32))
         nc.sync.dma_start(wbw[:].bitcast(I32), wb_words[0].bitcast(I32))
+        for dst, src in ((l_pv, offs5), (l_u, offs3), (l_pw, offs4)):
+            nc.sync.dma_start(dst[:], src)
         load_rows_direct(wcs, wc_scales)
-        nc.sync.dma_start(l_pv[:], offs5)
-        nc.sync.dma_start(l_u[:], offs3)
-        nc.sync.dma_start(l_pw[:], offs4)
         load_rows_direct(wbs, wb_scales)
 
-        for h in range(2):
-            nc.vector.tensor_copy(xs_all[64 * h : 64 * h + 64, :].bitcast(I32), xs_stage[:, h, :])
+        ww = tile("ww", [P, R], U16)
+        ws = tile("ws", [P, R], U8)
         xs = tile("xs", [P, J], U8)
         xw = tile("xw", [P, J], U32)
+        nc.vector.tensor_copy(ww[:], ww_all[:].indirect(l_r[:]))
         nc.vector.tensor_copy(xs[:], xs_all[:].indirect(l_j[:]))
         nc.vector.tensor_copy(xw[:], xw_all[:].indirect(l_j[:]))
         nc.vector.tensor_copy(w2s[64:128, 0, :].bitcast(I32), w2s[0:64, 1, :].bitcast(I32))
-
-        ww, ws = [], []
-        for h in range(2):
-            cols = slice(h * HALF_R // LIST_COL, (h + 1) * HALF_R // LIST_COL)
-            ww.append(tile(f"ww{h}", [P, HALF_R], U16))
-            nc.vector.tensor_copy(ww[h][:], ww_all[:].indirect(l_r[:, cols]))
-        for h in range(2):
-            cols = slice(h * HALF_R // LIST_COL, (h + 1) * HALF_R // LIST_COL)
-            ws.append(tile(f"ws{h}", [P, HALF_R], U8))
-            nc.vector.tensor_copy(ws[h][:], ws_all[:].indirect(l_r[:, cols]))
+        nc.vector.tensor_copy(ws[:], ws_all[:].indirect(l_r[:]))
 
         def x_side(jh):
             cols = slice(jh * P, (jh + 1) * P)
             return dict(lhsT=xw[:, cols].bitcast(E5M2), lhsT_scale=xs[:, cols])
 
         b_sb = []
-        for h in range(2):
-            cols = slice(h * HALF_R, (h + 1) * HALF_R)
-            b_ps = ps.tile([P, 2, HALF_R], F32, name=f"b_ps{h}", tag=f"bank_b{h}")
-            for jh in range(2):
-                nc.tensor.matmul_mx(b_ps[:, jh, :], rhs=w2w[:, cols].bitcast(E4M3), rhs_scale=w2s[:, 0, cols],
-                                    start=True, stop=True, **x_side(jh))
-            b_sb.append(tile(f"b_sb{h}", [P, 2, 2, 64, 2], F32))
-            nc.scalar.copy(b_sb[h][:], b_ps[:].rearrange("p j (m u e) -> p j u m e", u=2, e=2))
+        for jh in range(2):
+            b_ps = ps.tile([P, R], F32, name=f"b_ps{jh}", tag=f"bank_b{jh}")
+            nc.tensor.matmul_mx(b_ps[:], rhs=w2w[:].bitcast(E4M3), rhs_scale=w2s[:, 0, :],
+                                start=True, stop=True, **x_side(jh))
+            b_sb.append(tile(f"b_sb{jh}", [P, 2, P, 2], F32, tag=f"b_then_pw{jh}"))
+            nc.scalar.copy(b_sb[jh][:], b_ps[:].rearrange("p (m u e) -> p u m e", u=2, e=2))
 
         hid = [tile(f"hid{jh}", [P, 2, P, 2], BF16) for jh in range(2)]
-        for h in range(2):
-            a_ps = ps.tile([P, 2, HALF_R], F32, name=f"a_ps{h}", tag=f"bank_a{h}")
-            for jh in range(2):
-                nc.tensor.matmul_mx(a_ps[:, jh, :], rhs=ww[h][:].bitcast(E2M1), rhs_scale=ws[h][:],
-                                    start=True, stop=True, **x_side(jh))
-            for jh in range(2):
-                nc.vector.tensor_tensor(
-                    hid[jh][:, :, 64 * h : 64 * h + 64, :],
-                    a_ps[:, jh, :].rearrange("p (m u e) -> p u m e", u=2, e=2),
-                    b_sb[h][:, jh, :, :, :],
-                    mybir.AluOpType.max,
-                )
+        for jh in range(2):
+            a_ps = ps.tile([P, R], F32, name=f"a_ps{jh}", tag=f"bank_a{jh}0")
+            nc.tensor.matmul_mx(a_ps[:], rhs=ww[:].bitcast(E2M1), rhs_scale=ws[:],
+                                start=True, stop=True, **x_side(jh))
+            nc.vector.tensor_tensor(hid[jh][:], a_ps[:].rearrange("p (m u e) -> p u m e", u=2, e=2),
+                                    b_sb[jh][:], mybir.AluOpType.max)
+        pv.append(tile("pv1", [P, E], F32, tag="b_then_pw1"))
+        nc.vector.memset(pv[1][:], 0.0)
 
-        p_ps = [ps.tile([P, 2, P], F32, name=f"p_ps{n}", tag=f"bank_p{n}") for n in range(2)]
-        q_sb = []
+        q0_ps = ps.tile([P, 2, P], F32, name="q0_ps", tag="bank_q0")
+        late_ps = [ps.tile([P, 3, P], F32, name=f"late_ps{n}", tag=f"bank_late{n}") for n in range(2)]
         for jh in range(2):
             words = hid[jh][:].rearrange("p u m e -> p (u m e)").bitcast(F32)
             t_ps = ps.tile([P, 2, P], F32, name=f"t_ps{jh}", tag=f"bank_b{jh}")
             for u in range(2):
                 nc.tensor.transpose(t_ps[:, u, :], words[:, u * P : (u + 1) * P], ident[:])
-            hid_t = tile(f"hid_t{jh}", [P, 4 * P], BF16)
+            hid_t = tile(f"hid_t{jh}", [P, 4 * P], BF16, tag=f"hid_then_pw{jh}")
             nc.scalar.copy(hid_t[:].bitcast(F32).rearrange("p (j u) -> p j u", u=2), t_ps[:].rearrange("p u j -> p j u"))
             hw = tile(f"hw{jh}", [P, P], U32)
             hs = tile(f"hs{jh}", [P, P], U8)
             nc.vector.quantize_mx(hw[:].bitcast(E4M3), hs[:], hid_t[:])
+            pw.append(tile(f"pw{jh}", [P, E], F32, tag=f"hid_then_pw{jh}"))
+            nc.vector.memset(pw[jh][:], 0.0)
             h_side = dict(rhs=hw[:].bitcast(E4M3), rhs_scale=hs[:], start=True, stop=True)
-            q_ps = ps.tile([P, 2, P], F32, name=f"q_ps{jh}", tag=f"bank_q{jh}")
             for n in range(2):
                 cols = slice(n * P, (n + 1) * P)
-                nc.tensor.matmul_mx(q_ps[:, n, :], lhsT=wcw[:, cols].bitcast(E4M3), lhsT_scale=wcs[:, cols], **h_side)
+                q_dst = q0_ps[:, n, :] if jh == 0 else late_ps[n][:, 2, :]
+                nc.tensor.matmul_mx(q_dst, lhsT=wcw[:, cols].bitcast(E4M3), lhsT_scale=wcs[:, cols], **h_side)
             for n in range(2):
                 cols = slice(n * P, (n + 1) * P)
-                nc.tensor.matmul_mx(p_ps[n][:, jh, :], lhsT=wbw[:, 2 * n * P : 2 * (n + 1) * P].bitcast(E2M1),
+                nc.tensor.matmul_mx(late_ps[n][:, jh, :], lhsT=wbw[:, 2 * n * P : 2 * (n + 1) * P].bitcast(E2M1),
                                     lhsT_scale=wbs[:, cols], **h_side)
-            q_sb.append(tile(f"q_sb{jh}", [P, 2, P], F32))
-            nc.scalar.copy(q_sb[jh][:], q_ps[:])
+            if jh == 0:
+                q0_sb = tile("q0_sb", [P, 2, P], F32)
+                nc.scalar.copy(q0_sb[:], q0_ps[:])
+                nc.scalar.activation(pv[0][:].indirect(l_pv[:, 0:8]), q0_sb[:, 0, :], COPY)
+                nc.vector.tensor_copy(pv[1][:].indirect(l_pv[:, 0:8]), q0_sb[:, 1, :])
 
+        p_sb = [tile(f"p_sb{n}", [P, J], F32) for n in range(2)]
+        q1_sb = [tile(f"q1_sb{n}", [P, P], F32) for n in range(2)]
+        nc.scalar.copy(p_sb[0][:], late_ps[0][:, 0:2, :].rearrange("p h j -> p (h j)"))
+        nc.scalar.copy(q1_sb[0][:], late_ps[0][:, 2, :])
+        nc.vector.tensor_copy(q1_sb[1][:], late_ps[1][:, 2, :])
+        nc.vector.tensor_copy(p_sb[1][:], late_ps[1][:, 0:2, :].rearrange("p h j -> p (h j)"))
+        for n in (1, 0):
+            nc.vector.tensor_copy(pv[n][:].indirect(l_pv[:, 8:16]), q1_sb[n][:])
+        m0 = [tile(f"m0_{n}", [P, U], F32) for n in range(2)]
         for n in range(2):
-            p_sb = tile(f"p_sb{n}", [P, J], F32)
-            nc.scalar.copy(p_sb[:], p_ps[n][:].rearrange("p h j -> p (h j)"))
-            m0 = tile(f"m0_{n}", [P, U], F32)
-            nc.scalar.activation(m0[:], p_sb[:].indirect(l_u[:]), COPY, scale=q_sb[0][:, n, 0:1])
-            nc.scalar.activation(pw[n][:].indirect(l_pw[:]), m0[:], COPY)
-            for jh in range(2):
-                cols = slice(jh * P // LIST_COL, (jh + 1) * P // LIST_COL)
-                nc.vector.tensor_copy(pv[n][:].indirect(l_pv[:, cols]), q_sb[jh][:, n, :])
-            y = tile(f"y{n}", [P, E], F32)
-            nc.vector.tensor_tensor(y[:], pw[n][:], pv[n][:], mybir.AluOpType.add)
-            nc.sync.dma_start(out[n * P : (n + 1) * P, :], y[:])
+            nc.scalar.activation(m0[n][:], p_sb[n][:].indirect(l_u[:]), COPY, scale=q0_sb[:, n, 0:1])
+        for n in range(2):
+            nc.scalar.activation(pw[n][:].indirect(l_pw[:]), m0[n][:], COPY)
+        for n, pieces in ((0, 1), (1, 2)):
+            width = E // pieces
+            for c in range(pieces):
+                cols = slice(c * width, (c + 1) * width)
+                y = tile(f"y{n}{c}", [P, width], F32)
+                nc.vector.tensor_tensor(y[:], pw[n][:, cols], pv[n][:, cols], mybir.AluOpType.add)
+                nc.sync.dma_start(out[n * P : (n + 1) * P, cols], y[:])

@@ -49,7 +49,7 @@ def tile_list_outcomepages_storeleads_kernel(
         out_scales = tile("out_scales", [P, 2 * N], U8)
         wcs, wbs = out_scales[:, 0:N], out_scales[:, N : 2 * N]
         pv = [tile("pv0", [P, E], F32)]
-        pw = []
+        pw = [None, tile("pw1", [P, E], F32)]
         wcw = tile("wcw", [P, N], U32)
         wbw = tile("wbw", [P, 2 * N], U8)
         ident = tile("ident", [P, P], F32)
@@ -59,12 +59,13 @@ def tile_list_outcomepages_storeleads_kernel(
         nc.vector.memset(ws_all[:].bitcast(I32), 0)
         nc.vector.memset(out_scales[:].bitcast(I32), 0)
         nc.vector.memset(pv[0][:], 0.0)
+        nc.vector.memset(pw[1][:], 0.0)
         make_identity(nc, ident[:])
 
-        def load_rows_direct(plane, scales):
+        def load_rows_direct(plane, scales, quadrants=range(4), queue=nc.sync):
             rows = scales[0].bitcast(I32)
-            for q in range(4):
-                nc.sync.dma_start(plane[32 * q : 32 * q + 4, :].bitcast(I32), rows[4 * q : 4 * q + 4, :])
+            for q in quadrants:
+                queue.dma_start(plane[32 * q : 32 * q + 4, :].bitcast(I32), rows[4 * q : 4 * q + 4, :])
 
         def load_rows_paired(stage, scales):
             rows = scales[0].bitcast(I32).rearrange("(h q r) c -> q r h c", h=2, q=2)
@@ -74,7 +75,8 @@ def tile_list_outcomepages_storeleads_kernel(
         nc.sync.dma_start(l_r[:], offs)
         nc.sync.dma_start(ww_all[:].bitcast(I32), wt_words[0].bitcast(I32))
         nc.sync.dma_start(l_j[:], offs2)
-        load_rows_direct(xs_all, xt_scales)
+        load_rows_direct(xs_all, xt_scales, (0, 1), nc.scalar)
+        load_rows_direct(xs_all, xt_scales, (2, 3))
         nc.sync.dma_start(xw_all[:].bitcast(I32), xt_words[0].rearrange("p c t -> p (c t)").bitcast(I32))
         nc.sync.dma_start(w2w[:].bitcast(I32), w2_words[0].rearrange("p c t -> p (c t)").bitcast(I32))
         load_rows_paired(w2s[:].bitcast(I32), w2_scales)
@@ -108,56 +110,58 @@ def tile_list_outcomepages_storeleads_kernel(
             b_sb.append(tile(f"b_sb{jh}", [P, 2, P, 2], F32, tag=f"b_then_pw{jh}"))
             nc.scalar.copy(b_sb[jh][:], b_ps[:].rearrange("p (m u e) -> p u m e", u=2, e=2))
 
-        hid = [tile(f"hid{jh}", [P, 2, P, 2], BF16) for jh in range(2)]
+        hid = [[tile(f"hid{jh}{u}", [P, P, 2], BF16) for u in range(2)] for jh in range(2)]
         for jh in range(2):
             a_ps = ps.tile([P, R], F32, name=f"a_ps{jh}", tag=f"bank_a{jh}0")
             nc.tensor.matmul_mx(a_ps[:], rhs=ww[:].bitcast(E2M1), rhs_scale=ws[:],
                                 start=True, stop=True, **x_side(jh))
-            nc.vector.tensor_tensor(hid[jh][:], a_ps[:].rearrange("p (m u e) -> p u m e", u=2, e=2),
-                                    b_sb[jh][:], mybir.AluOpType.max)
+            for u in range(2):
+                nc.vector.tensor_tensor(hid[jh][u][:], a_ps[:].rearrange("p (m u e) -> p u m e", u=2, e=2)[:, u],
+                                        b_sb[jh][:, u], mybir.AluOpType.max)
         pv.append(tile("pv1", [P, E], F32, tag="b_then_pw1"))
         nc.vector.memset(pv[1][:], 0.0)
 
-        q0_ps = ps.tile([P, 2, P], F32, name="q0_ps", tag="bank_q0")
+        q0_ps = [ps.tile([P, P], F32, name=f"q0_ps{n}", tag=f"bank_q{n}") for n in range(2)]
         late_ps = [ps.tile([P, 3, P], F32, name=f"late_ps{n}", tag=f"bank_late{n}") for n in range(2)]
         for jh in range(2):
-            words = hid[jh][:].rearrange("p u m e -> p (u m e)").bitcast(F32)
             t_ps = ps.tile([P, 2, P], F32, name=f"t_ps{jh}", tag=f"bank_b{jh}")
             for u in range(2):
-                nc.tensor.transpose(t_ps[:, u, :], words[:, u * P : (u + 1) * P], ident[:])
+                nc.tensor.transpose(t_ps[:, u, :], hid[jh][u][:].rearrange("p m e -> p (m e)").bitcast(F32), ident[:])
             hid_t = tile(f"hid_t{jh}", [P, 4 * P], BF16, tag=f"hid_then_pw{jh}")
             nc.scalar.copy(hid_t[:].bitcast(F32).rearrange("p (j u) -> p j u", u=2), t_ps[:].rearrange("p u j -> p j u"))
             hw = tile(f"hw{jh}", [P, P], U32)
             hs = tile(f"hs{jh}", [P, P], U8)
             nc.vector.quantize_mx(hw[:].bitcast(E4M3), hs[:], hid_t[:])
-            pw.append(tile(f"pw{jh}", [P, E], F32, tag=f"hid_then_pw{jh}"))
-            nc.vector.memset(pw[jh][:], 0.0)
+            if jh == 0:
+                pw[0] = tile("pw0", [P, E], F32, tag="hid_then_pw0")
+                nc.vector.memset(pw[0][:], 0.0)
             h_side = dict(rhs=hw[:].bitcast(E4M3), rhs_scale=hs[:], start=True, stop=True)
             for n in range(2):
                 cols = slice(n * P, (n + 1) * P)
-                q_dst = q0_ps[:, n, :] if jh == 0 else late_ps[n][:, 2, :]
+                q_dst = q0_ps[n][:] if jh == 0 else late_ps[1 - n][:, 2, :]
                 nc.tensor.matmul_mx(q_dst, lhsT=wcw[:, cols].bitcast(E4M3), lhsT_scale=wcs[:, cols], **h_side)
             for n in range(2):
                 cols = slice(n * P, (n + 1) * P)
                 nc.tensor.matmul_mx(late_ps[n][:, jh, :], lhsT=wbw[:, 2 * n * P : 2 * (n + 1) * P].bitcast(E2M1),
                                     lhsT_scale=wbs[:, cols], **h_side)
             if jh == 0:
-                q0_sb = tile("q0_sb", [P, 2, P], F32)
-                nc.scalar.copy(q0_sb[:], q0_ps[:])
-                nc.scalar.activation(pv[0][:].indirect(l_pv[:, 0:8]), q0_sb[:, 0, :], COPY)
-                nc.vector.tensor_copy(pv[1][:].indirect(l_pv[:, 0:8]), q0_sb[:, 1, :])
+                q0_sb = [tile(f"q0_sb{n}", [P, P], F32) for n in range(2)]
+                nc.vector.tensor_copy(q0_sb[0][:], q0_ps[0][:])
+                nc.scalar.copy(q0_sb[1][:], q0_ps[1][:])
+                nc.scalar.activation(pv[0][:].indirect(l_pv[:, 0:8]), q0_sb[0][:], COPY)
+                nc.vector.tensor_copy(pv[1][:].indirect(l_pv[:, 0:8]), q0_sb[1][:])
 
         p_sb = [tile(f"p_sb{n}", [P, J], F32) for n in range(2)]
         q1_sb = [tile(f"q1_sb{n}", [P, P], F32) for n in range(2)]
         nc.scalar.copy(p_sb[0][:], late_ps[0][:, 0:2, :].rearrange("p h j -> p (h j)"))
-        nc.scalar.copy(q1_sb[0][:], late_ps[0][:, 2, :])
-        nc.vector.tensor_copy(q1_sb[1][:], late_ps[1][:, 2, :])
+        nc.scalar.copy(q1_sb[1][:], late_ps[0][:, 2, :])
+        nc.vector.tensor_copy(q1_sb[0][:], late_ps[1][:, 2, :])
         nc.vector.tensor_copy(p_sb[1][:], late_ps[1][:, 0:2, :].rearrange("p h j -> p (h j)"))
-        for n in (1, 0):
+        for n in range(2):
             nc.vector.tensor_copy(pv[n][:].indirect(l_pv[:, 8:16]), q1_sb[n][:])
         m0 = [tile(f"m0_{n}", [P, U], F32) for n in range(2)]
         for n in range(2):
-            nc.scalar.activation(m0[n][:], p_sb[n][:].indirect(l_u[:]), COPY, scale=q0_sb[:, n, 0:1])
+            nc.scalar.activation(m0[n][:], p_sb[n][:].indirect(l_u[:]), COPY, scale=q0_sb[n][:, 0:1])
         for n in range(2):
             nc.scalar.activation(pw[n][:].indirect(l_pw[:]), m0[n][:], COPY)
         for n, pieces in ((0, 1), (1, 2)):

@@ -48,8 +48,8 @@ def tile_list_outcomepages_storeleads_kernel(
         w2w = tile("w2w", [P, R], U32)
         out_scales = tile("out_scales", [P, 2 * N], U8)
         wcs, wbs = out_scales[:, 0:N], out_scales[:, N : 2 * N]
-        pv = [tile("pv0", [P, E], F32)]
-        pw = [None, tile("pw1", [P, E], F32)]
+        pv = [tile(f"pv{n}", [P, E], F32) for n in range(2)]
+        pw = [tile(f"pw{n}", [P, E], F32) for n in range(2)]
         wcw = tile("wcw", [P, N], U32)
         wbw = tile("wbw", [P, 2 * N], U8)
         ident = tile("ident", [P, P], F32)
@@ -58,8 +58,8 @@ def tile_list_outcomepages_storeleads_kernel(
         nc.vector.memset(w2s[:].rearrange("p h c -> p (h c)").bitcast(I32), 0)
         nc.vector.memset(ws_all[:].bitcast(I32), 0)
         nc.vector.memset(out_scales[:].bitcast(I32), 0)
-        nc.vector.memset(pv[0][:], 0.0)
-        nc.vector.memset(pw[1][:], 0.0)
+        for page in pv + pw:
+            nc.vector.memset(page[:], 0.0)
         make_identity(nc, ident[:])
 
         def load_rows_direct(plane, scales, quadrants=range(4), queue=nc.sync):
@@ -107,7 +107,7 @@ def tile_list_outcomepages_storeleads_kernel(
             b_ps = ps.tile([P, R], F32, name=f"b_ps{jh}", tag=f"bank_b{jh}")
             nc.tensor.matmul_mx(b_ps[:], rhs=w2w[:].bitcast(E4M3), rhs_scale=w2s[:, 0, :],
                                 start=True, stop=True, **x_side(jh))
-            b_sb.append(tile(f"b_sb{jh}", [P, 2, P, 2], F32, tag=f"b_then_pw{jh}"))
+            b_sb.append(tile(f"b_sb{jh}", [P, 2, P, 2], F32))
             nc.scalar.copy(b_sb[jh][:], b_ps[:].rearrange("p (m u e) -> p u m e", u=2, e=2))
 
         hid = [[tile(f"hid{jh}{u}", [P, P, 2], BF16) for u in range(2)] for jh in range(2)]
@@ -118,8 +118,6 @@ def tile_list_outcomepages_storeleads_kernel(
             for u in range(2):
                 nc.vector.tensor_tensor(hid[jh][u][:], a_ps[:].rearrange("p (m u e) -> p u m e", u=2, e=2)[:, u],
                                         b_sb[jh][:, u], mybir.AluOpType.max)
-        pv.append(tile("pv1", [P, E], F32, tag="b_then_pw1"))
-        nc.vector.memset(pv[1][:], 0.0)
 
         q0_ps = [ps.tile([P, P], F32, name=f"q0_ps{n}", tag=f"bank_q{n}") for n in range(2)]
         late_ps = [ps.tile([P, 3, P], F32, name=f"late_ps{n}", tag=f"bank_late{n}") for n in range(2)]
@@ -127,14 +125,11 @@ def tile_list_outcomepages_storeleads_kernel(
             t_ps = ps.tile([P, 2, P], F32, name=f"t_ps{jh}", tag=f"bank_b{jh}")
             for u in range(2):
                 nc.tensor.transpose(t_ps[:, u, :], hid[jh][u][:].rearrange("p m e -> p (m e)").bitcast(F32), ident[:])
-            hid_t = tile(f"hid_t{jh}", [P, 4 * P], BF16, tag=f"hid_then_pw{jh}")
+            hid_t = tile(f"hid_t{jh}", [P, 4 * P], BF16)
             nc.scalar.copy(hid_t[:].bitcast(F32).rearrange("p (j u) -> p j u", u=2), t_ps[:].rearrange("p u j -> p j u"))
             hw = tile(f"hw{jh}", [P, P], U32)
             hs = tile(f"hs{jh}", [P, P], U8)
             nc.vector.quantize_mx(hw[:].bitcast(E4M3), hs[:], hid_t[:])
-            if jh == 0:
-                pw[0] = tile("pw0", [P, E], F32, tag="hid_then_pw0")
-                nc.vector.memset(pw[0][:], 0.0)
             h_side = dict(rhs=hw[:].bitcast(E4M3), rhs_scale=hs[:], start=True, stop=True)
             for n in range(2):
                 cols = slice(n * P, (n + 1) * P)
@@ -146,7 +141,7 @@ def tile_list_outcomepages_storeleads_kernel(
                                     lhsT_scale=wbs[:, cols], **h_side)
             if jh == 0:
                 q0_sb = [tile(f"q0_sb{n}", [P, P], F32) for n in range(2)]
-                nc.vector.tensor_copy(q0_sb[0][:], q0_ps[0][:])
+                nc.scalar.copy(q0_sb[0][:], q0_ps[0][:])
                 nc.scalar.copy(q0_sb[1][:], q0_ps[1][:])
                 nc.scalar.activation(pv[0][:].indirect(l_pv[:, 0:8]), q0_sb[0][:], COPY)
                 nc.vector.tensor_copy(pv[1][:].indirect(l_pv[:, 0:8]), q0_sb[1][:])

from contextlib import ExitStack

import concourse.mybir as mybir
from concourse.masks import make_identity

K, T, J, R, V, N, U, E = 512, 1024, 256, 512, 1024, 256, 128, 512
FLOPS = 2 * (2 * K * R * J + 2 * R * N * J)

F32 = mybir.dt.float32
BF16 = mybir.dt.bfloat16
I32 = mybir.dt.int32
U32 = mybir.dt.uint32
U16 = mybir.dt.uint16
U8 = mybir.dt.uint8
E4M3 = mybir.dt.float8_e4m3fn_x4
E5M2 = mybir.dt.float8_e5m2_x4
E2M1 = mybir.dt.float4_e2m1fn_x4
COPY = mybir.ActivationFunctionType.Copy

P = 128
HALF_R = R // 2
LIST_COL = 16


def tile_list_outcomepages_storeleads_kernel(
    tc, xt_words, xt_scales, wt_words, wt_scales, w2_words, w2_scales,
    wb_words, wb_scales, wc_words, wc_scales, offs, offs2, offs3, offs4, offs5, out,
):
    nc = tc.nc
    with ExitStack() as ctx:
        sb = ctx.enter_context(tc.tile_pool(name="sb", bufs=1))
        ps = ctx.enter_context(tc.psum_pool(name="ps", bufs=1))

        def tile(name, shape, dtype, tag=None):
            return sb.tile(shape, dtype, name=name, tag=tag or name, align_bytes=64)

        l_r = tile("l_r", [P, R // LIST_COL], U16)
        l_j = tile("l_j", [P, J // LIST_COL], U16)
        l_u = tile("l_u", [P, U // LIST_COL], U16)
        l_pw = tile("l_pw", [P, U // LIST_COL], U16)
        l_pv = tile("l_pv", [P, J // LIST_COL], U16)

        xs_all = tile("xs_all", [P, T], U8)
        xw_all = tile("xw_all", [P, T], U32)
        ws_all = tile("ws_all", [P, V], U8)
        ww_all = tile("ww_all", [P, V], U16)
        w2s = tile("w2s", [P, 2, R], U8)
        w2w = tile("w2w", [P, R], U32)
        out_scales = tile("out_scales", [P, 2 * N], U8)
        wcs, wbs = out_scales[:, 0:N], out_scales[:, N : 2 * N]
        pv = [tile(f"pv{n}", [P, E], F32) for n in range(2)]
        pw = [tile(f"pw{n}", [P, E], F32) for n in range(2)]
        wcw = tile("wcw", [P, N], U32)
        wbw = tile("wbw", [P, 2 * N], U8)
        ident = tile("ident", [P, P], F32)

        nc.vector.memset(xs_all[:].bitcast(I32), 0)
        nc.vector.memset(w2s[:].rearrange("p h c -> p (h c)").bitcast(I32), 0)
        nc.vector.memset(ws_all[:].bitcast(I32), 0)
        nc.vector.memset(out_scales[:].bitcast(I32), 0)
        for page in pv + pw:
            nc.vector.memset(page[:], 0.0)
        make_identity(nc, ident[:])

        def load_rows_direct(plane, scales, quadrants=range(4), queue=nc.sync):
            rows = scales[0].bitcast(I32)
            for q in quadrants:
                queue.dma_start(plane[32 * q : 32 * q + 4, :].bitcast(I32), rows[4 * q : 4 * q + 4, :])

        def load_rows_paired(stage, scales):
            rows = scales[0].bitcast(I32).rearrange("(h q r) c -> q r h c", h=2, q=2)
            for q in range(2):
                nc.sync.dma_start(stage[32 * q : 32 * q + 4, :, :], rows[q])

        nc.sync.dma_start(l_r[:], offs)
        nc.sync.dma_start(ww_all[:].bitcast(I32), wt_words[0].bitcast(I32))
        nc.sync.dma_start(l_j[:], offs2)
        load_rows_direct(xs_all, xt_scales, (0, 1), nc.scalar)
        load_rows_direct(xs_all, xt_scales, (2, 3))
        nc.sync.dma_start(xw_all[:].bitcast(I32), xt_words[0].rearrange("p c t -> p (c t)").bitcast(I32))
        nc.sync.dma_start(w2w[:].bitcast(I32), w2_words[0].rearrange("p c t -> p (c t)").bitcast(I32))
        load_rows_paired(w2s[:].bitcast(I32), w2_scales)
        load_rows_direct(ws_all, wt_scales)
        nc.sync.dma_start(wcw[:].bitcast(I32), wc_words[0].rearrange("p c t -> p (c t)").bitcast(I32))
        nc.sync.dma_start(wbw[:].bitcast(I32), wb_words[0].bitcast(I32))
        for dst, src in ((l_pv, offs5), (l_u, offs3), (l_pw, offs4)):
            nc.sync.dma_start(dst[:], src)
        load_rows_direct(wcs, wc_scales)
        load_rows_direct(wbs, wb_scales)

        ww = tile("ww", [P, R], U16)
        ws = tile("ws", [P, R], U8)
        xs = tile("xs", [P, J], U8)
        xw = tile("xw", [P, J], U32)
        nc.vector.tensor_copy(ww[:], ww_all[:].indirect(l_r[:]))
        nc.vector.tensor_copy(xs[:], xs_all[:].indirect(l_j[:]))
        nc.vector.tensor_copy(xw[:], xw_all[:].indirect(l_j[:]))
        nc.vector.tensor_copy(w2s[64:128, 0, :].bitcast(I32), w2s[0:64, 1, :].bitcast(I32))
        nc.vector.tensor_copy(ws[:], ws_all[:].indirect(l_r[:]))

        def x_side(jh):
            cols = slice(jh * P, (jh + 1) * P)
            return dict(lhsT=xw[:, cols].bitcast(E5M2), lhsT_scale=xs[:, cols])

        b_sb = []
        for jh in range(2):
            b_ps = ps.tile([P, R], F32, name=f"b_ps{jh}", tag=f"bank_b{jh}")
            nc.tensor.matmul_mx(b_ps[:], rhs=w2w[:].bitcast(E4M3), rhs_scale=w2s[:, 0, :],
                                start=True, stop=True, **x_side(jh))
            b_sb.append(tile(f"b_sb{jh}", [P, 2, P, 2], F32))
            nc.scalar.copy(b_sb[jh][:], b_ps[:].rearrange("p (m u e) -> p u m e", u=2, e=2))

        hid = [[tile(f"hid{jh}{u}", [P, P, 2], BF16) for u in range(2)] for jh in range(2)]
        for jh in range(2):
            a_ps = ps.tile([P, R], F32, name=f"a_ps{jh}", tag=f"bank_a{jh}0")
            nc.tensor.matmul_mx(a_ps[:], rhs=ww[:].bitcast(E2M1), rhs_scale=ws[:],
                                start=True, stop=True, **x_side(jh))
            for u in range(2):
                nc.vector.tensor_tensor(hid[jh][u][:], a_ps[:].rearrange("p (m u e) -> p u m e", u=2, e=2)[:, u],
                                        b_sb[jh][:, u], mybir.AluOpType.max)

        q0_ps = [ps.tile([P, P], F32, name=f"q0_ps{n}", tag=f"bank_q{n}") for n in range(2)]
        late_ps = [ps.tile([P, 3, P], F32, name=f"late_ps{n}", tag=f"bank_late{n}") for n in range(2)]
        for jh in range(2):
            t_ps = ps.tile([P, 2, P], F32, name=f"t_ps{jh}", tag=f"bank_b{jh}")
            for u in range(2):
                nc.tensor.transpose(t_ps[:, u, :], hid[jh][u][:].rearrange("p m e -> p (m e)").bitcast(F32), ident[:])
            hid_t = tile(f"hid_t{jh}", [P, 4 * P], BF16)
            nc.scalar.copy(hid_t[:].bitcast(F32).rearrange("p (j u) -> p j u", u=2), t_ps[:].rearrange("p u j -> p j u"))
            hw = tile(f"hw{jh}", [P, P], U32)
            hs = tile(f"hs{jh}", [P, P], U8)
            nc.vector.quantize_mx(hw[:].bitcast(E4M3), hs[:], hid_t[:])
            h_side = dict(rhs=hw[:].bitcast(E4M3), rhs_scale=hs[:], start=True, stop=True)
            for n in range(2):
                cols = slice(n * P, (n + 1) * P)
                q_dst = q0_ps[n][:] if jh == 0 else late_ps[1 - n][:, 2, :]
                nc.tensor.matmul_mx(q_dst, lhsT=wcw[:, cols].bitcast(E4M3), lhsT_scale=wcs[:, cols], **h_side)
            for n in range(2):
                cols = slice(n * P, (n + 1) * P)
                nc.tensor.matmul_mx(late_ps[n][:, jh, :], lhsT=wbw[:, 2 * n * P : 2 * (n + 1) * P].bitcast(E2M1),
                                    lhsT_scale=wbs[:, cols], **h_side)
            if jh == 0:
                q0_sb = [tile(f"q0_sb{n}", [P, P], F32) for n in range(2)]
                nc.scalar.copy(q0_sb[0][:], q0_ps[0][:])
                nc.scalar.copy(q0_sb[1][:], q0_ps[1][:])
                nc.scalar.activation(pv[0][:].indirect(l_pv[:, 0:8]), q0_sb[0][:], COPY)
                nc.vector.tensor_copy(pv[1][:].indirect(l_pv[:, 0:8]), q0_sb[1][:])

        p_sb = [tile(f"p_sb{n}", [P, J], F32) for n in range(2)]
        q1_sb = [tile(f"q1_sb{n}", [P, P], F32) for n in range(2)]
        nc.scalar.copy(p_sb[0][:], late_ps[0][:, 0:2, :].rearrange("p h j -> p (h j)"))
        nc.scalar.copy(q1_sb[1][:], late_ps[0][:, 2, :])
        nc.vector.tensor_copy(q1_sb[0][:], late_ps[1][:, 2, :])
        nc.vector.tensor_copy(p_sb[1][:], late_ps[1][:, 0:2, :].rearrange("p h j -> p (h j)"))
        for n in range(2):
            nc.vector.tensor_copy(pv[n][:].indirect(l_pv[:, 8:16]), q1_sb[n][:])
        m0 = [tile(f"m0_{n}", [P, U], F32) for n in range(2)]
        for n in range(2):
            nc.scalar.activation(m0[n][:], p_sb[n][:].indirect(l_u[:]), COPY, scale=q0_sb[n][:, 0:1])
        for n in range(2):
            nc.scalar.activation(pw[n][:].indirect(l_pw[:]), m0[n][:], COPY)
        for n, pieces in ((0, 1), (1, 2)):
            width = E // pieces
            for c in range(pieces):
                cols = slice(c * width, (c + 1) * width)
                y = tile(f"y{n}{c}", [P, width], F32)
                nc.vector.tensor_tensor(y[:], pw[n][:, cols], pv[n][:, cols], mybir.AluOpType.add)
                nc.sync.dma_start(out[n * P : (n + 1) * P, cols], y[:])
